import numpy as np
import ml_dtypes

BF16 = ml_dtypes.bfloat16


def bf(x):
    return np.asarray(x, np.float32).astype(BF16)


def f32(x):
    return np.asarray(x, np.float32)


def f64(x):
    return np.asarray(x).astype(np.float64)


def striped(idx):
    return np.tile(idx.reshape(-1, 16).T, (8, 1))


S, K, M, N, B, Q = 512, 512, 256, 512, 2, 256


def gelu_tanh(v):
    return 0.5 * v * (1.0 + np.tanh(np.sqrt(2.0 / np.pi) * (v + 0.044715 * v**3)))


def setup_inputs():
    return {"base": bf(np.random.standard_normal((B, M, S))), "x": bf(np.random.standard_normal((K, N))), "w": bf(np.random.standard_normal((K, M)) / np.sqrt(K)), "b": f32(0.5 * np.random.standard_normal((M, 1))), "offs": striped(np.random.permutation(S))}


def reference(base, x, w, b, offs):
    idx = offs[:16].T.reshape(-1)
    z = f64(base).copy()
    for i in range(B):
        z[i][:, idx[i * Q : (i + 1) * Q]] += f64(w).T @ f64(x)[:, i * Q : (i + 1) * Q]
    return gelu_tanh(z + f64(b))

@@ -1,0 +1,61 @@
+import concourse.mybir as mybir
+from concourse.masks import make_identity
+
+BF16, F32, U16 = mybir.dt.bfloat16, mybir.dt.float32, mybir.dt.uint16
+GELU = mybir.ActivationFunctionType.Gelu_apprx_tanh
+
+P = 128
+SEQS, FEATS, TOKENS = 2, 256, 512
+K, N = 512, 512
+PIECE = N // SEQS
+K_BLOCKS = K // P
+FEAT_BLOCKS = FEATS // P
+OFFS_COLS = PIECE // 16
+
+FLOPS = 2 * K * FEATS * N
+
+
+def tile_scatter_matmul_kernel(tc, base, x, w, b, offs, out):
+    nc = tc.nc
+    with (
+        tc.tile_pool(name="held", bufs=1) as held,
+        tc.tile_pool(name="results", bufs=SEQS * FEAT_BLOCKS) as results,
+        tc.psum_pool(name="windows", bufs=1) as windows,
+    ):
+        offsets = held.tile([P, N // 16], U16, name="offsets")
+        nc.sync.dma_start(offsets[:], offs)
+
+        base_sb = held.tile([P, SEQS * FEAT_BLOCKS, TOKENS], BF16, name="base_sb")
+        nc.scalar.dma_start(base_sb[:], base.rearrange("i (a p) t -> p (i a) t", p=P))
+        x_sb = held.tile([P, K_BLOCKS, N], BF16, name="x_sb")
+        nc.sync.dma_start(x_sb[:], x.rearrange("(kb p) n -> p kb n", p=P))
+        w_sb = held.tile([P, K_BLOCKS, FEATS], BF16, name="w_sb")
+        nc.gpsimd.dma_start(w_sb[:], w.rearrange("(kb p) m -> p kb m", p=P))
+        bias = held.tile([P, FEAT_BLOCKS], F32, name="bias")
+        nc.scalar.dma_start(bias[:], b.rearrange("(a p) o -> p (a o)", p=P))
+
+        ident = held.tile([P, P], BF16, name="ident")
+        make_identity(nc, ident[:])
+
+        blocks = [(i, a) for i in range(SEQS) for a in range(FEAT_BLOCKS)]
+
+        window = {}
+        for i, a in blocks:
+            window[i, a] = windows.tile([P, TOKENS], F32, name="window_%d_%d" % (i, a))
+            nc.tensor.matmul(
+                window[i, a][:], ident[:], base_sb[:, i * FEAT_BLOCKS + a, :],
+                start=True, stop=False,
+            )
+
+        for i, a in blocks:
+            places = offsets[:, i * OFFS_COLS : (i + 1) * OFFS_COLS]
+            for kb in range(K_BLOCKS):
+                nc.tensor.matmul(
+                    window[i, a][:].indirect(places),
+                    w_sb[:, kb, a * P : (a + 1) * P],
+                    x_sb[:, kb, i * PIECE : (i + 1) * PIECE],
+                    start=False, stop=(kb == K_BLOCKS - 1),
+                )
+            result = results.tile([P, TOKENS], F32, name="result")
+            nc.scalar.activation(result[:], window[i, a][:], GELU, bias=bias[:, a : a + 1])
+            nc.sync.dma_start(out[i, a * P : (a + 1) * P, :], result[:])

@@ -17,6 +17,7 @@ FLOPS = 2 * K * FEATS * N
 
 def tile_scatter_matmul_kernel(tc, base, x, w, b, offs, out):
     nc = tc.nc
+    blocks = [(i, a) for i in range(SEQS) for a in range(FEAT_BLOCKS)]
     with (
         tc.tile_pool(name="held", bufs=1) as held,
         tc.tile_pool(name="results", bufs=SEQS * FEAT_BLOCKS) as results,
@@ -25,35 +26,43 @@ def tile_scatter_matmul_kernel(tc, base, x, w, b, offs, out):
         offsets = held.tile([P, N // 16], U16, name="offsets")
         nc.sync.dma_start(offsets[:], offs)
 
-        base_sb = held.tile([P, SEQS * FEAT_BLOCKS, TOKENS], BF16, name="base_sb")
-        nc.scalar.dma_start(base_sb[:], base.rearrange("i (a p) t -> p (i a) t", p=P))
-        x_sb = held.tile([P, K_BLOCKS, N], BF16, name="x_sb")
-        nc.sync.dma_start(x_sb[:], x.rearrange("(kb p) n -> p kb n", p=P))
-        w_sb = held.tile([P, K_BLOCKS, FEATS], BF16, name="w_sb")
-        nc.gpsimd.dma_start(w_sb[:], w.rearrange("(kb p) m -> p kb m", p=P))
-        bias = held.tile([P, FEAT_BLOCKS], F32, name="bias")
-        nc.scalar.dma_start(bias[:], b.rearrange("(a p) o -> p (a o)", p=P))
-
         ident = held.tile([P, P], BF16, name="ident")
         make_identity(nc, ident[:])
 
-        blocks = [(i, a) for i in range(SEQS) for a in range(FEAT_BLOCKS)]
+        base_sb = {(i, a): held.tile([P, TOKENS], BF16, name="base_sb_%d_%d" % (i, a)) for i, a in blocks}
+        w_sb = [held.tile([P, FEATS], BF16, name="w_sb_%d" % kb) for kb in range(K_BLOCKS)]
+        x_sb = {
+            (i, kb): held.tile([P, PIECE], BF16, name="x_sb_%d_%d" % (i, kb))
+            for i in range(SEQS) for kb in range(K_BLOCKS)
+        }
+        loads = [(base_sb[i, a], base[i, a * P : (a + 1) * P, :]) for i, a in blocks]
+        for kb in range(K_BLOCKS):
+            loads.append((w_sb[kb], w[kb * P : (kb + 1) * P, :]))
+            loads.append((x_sb[0, kb], x[kb * P : (kb + 1) * P, 0:PIECE]))
+        for kb in range(K_BLOCKS):
+            loads.append((x_sb[1, kb], x[kb * P : (kb + 1) * P, PIECE : 2 * PIECE]))
+        for tile, source in loads:
+            nc.sync.dma_start(tile[:], source)
+        bias = held.tile([P, FEAT_BLOCKS], F32, name="bias")
+        nc.gpsimd.dma_start(bias[:], b.rearrange("(a p) o -> p (a o)", p=P))
+
+        zeros = held.tile([P, 1], F32, name="zeros")
+        nc.vector.memset(zeros[:], 0.0)
+        warmed = held.tile([P, 1], F32, name="warmed")
+        nc.scalar.activation(warmed[:], zeros[:], GELU)
 
         window = {}
         for i, a in blocks:
             window[i, a] = windows.tile([P, TOKENS], F32, name="window_%d_%d" % (i, a))
-            nc.tensor.matmul(
-                window[i, a][:], ident[:], base_sb[:, i * FEAT_BLOCKS + a, :],
-                start=True, stop=False,
-            )
+            nc.tensor.matmul(window[i, a][:], ident[:], base_sb[i, a][:], start=True, stop=False)
 
         for i, a in blocks:
             places = offsets[:, i * OFFS_COLS : (i + 1) * OFFS_COLS]
             for kb in range(K_BLOCKS):
                 nc.tensor.matmul(
                     window[i, a][:].indirect(places),
-                    w_sb[:, kb, a * P : (a + 1) * P],
-                    x_sb[:, kb, i * PIECE : (i + 1) * PIECE],
+                    w_sb[kb][:, a * P : (a + 1) * P],
+                    x_sb[i, kb][:],
                     start=False, stop=(kb == K_BLOCKS - 1),
                 )
             result = results.tile([P, TOKENS], F32, name="result")

@@ -12,6 +12,8 @@ K_BLOCKS = K // P
 FEAT_BLOCKS = FEATS // P
 OFFS_COLS = PIECE // 16
 
+WARM_UPS = 4
+
 FLOPS = 2 * K * FEATS * N
 
 
@@ -46,10 +48,13 @@ def tile_scatter_matmul_kernel(tc, base, x, w, b, offs, out):
         bias = held.tile([P, FEAT_BLOCKS], F32, name="bias")
         nc.gpsimd.dma_start(bias[:], b.rearrange("(a p) o -> p (a o)", p=P))
 
-        zeros = held.tile([P, 1], F32, name="zeros")
+        zeros = held.tile([P, TOKENS], BF16, name="zeros")
         nc.vector.memset(zeros[:], 0.0)
-        warmed = held.tile([P, 1], F32, name="warmed")
-        nc.scalar.activation(warmed[:], zeros[:], GELU)
+        idle_gelu = held.tile([P, 1], F32, name="idle_gelu")
+        nc.scalar.activation(idle_gelu[:], zeros[:, 0:1], GELU)
+        idle_bank = windows.tile([P, TOKENS], F32, name="idle_bank")
+        for repeat in range(WARM_UPS):
+            nc.tensor.matmul(idle_bank[:], zeros[:, 0:P], zeros[:], start=True, stop=True)
 
         window = {}
         for i, a in blocks:

@@ -26,7 +26,6 @@ def tile_scatter_matmul_kernel(tc, base, x, w, b, offs, out):
         tc.psum_pool(name="windows", bufs=1) as windows,
     ):
         offsets = held.tile([P, N // 16], U16, name="offsets")
-        nc.sync.dma_start(offsets[:], offs)
 
         ident = held.tile([P, P], BF16, name="ident")
         make_identity(nc, ident[:])
@@ -38,15 +37,16 @@ def tile_scatter_matmul_kernel(tc, base, x, w, b, offs, out):
             for i in range(SEQS) for kb in range(K_BLOCKS)
         }
         loads = [(base_sb[i, a], base[i, a * P : (a + 1) * P, :]) for i, a in blocks]
+        loads.append((offsets, offs))
         for kb in range(K_BLOCKS):
             loads.append((w_sb[kb], w[kb * P : (kb + 1) * P, :]))
             loads.append((x_sb[0, kb], x[kb * P : (kb + 1) * P, 0:PIECE]))
+        bias = held.tile([P, FEAT_BLOCKS], F32, name="bias")
+        loads.append((bias, b.rearrange("(a p) o -> p (a o)", p=P)))
         for kb in range(K_BLOCKS):
             loads.append((x_sb[1, kb], x[kb * P : (kb + 1) * P, PIECE : 2 * PIECE]))
         for tile, source in loads:
             nc.sync.dma_start(tile[:], source)
-        bias = held.tile([P, FEAT_BLOCKS], F32, name="bias")
-        nc.gpsimd.dma_start(bias[:], b.rearrange("(a p) o -> p (a o)", p=P))
 
         zeros = held.tile([P, TOKENS], BF16, name="zeros")
         nc.vector.memset(zeros[:], 0.0)

@@ -61,15 +61,25 @@ def tile_scatter_matmul_kernel(tc, base, x, w, b, offs, out):
             window[i, a] = windows.tile([P, TOKENS], F32, name="window_%d_%d" % (i, a))
             nc.tensor.matmul(window[i, a][:], ident[:], base_sb[i, a][:], start=True, stop=False)
 
-        for i, a in blocks:
-            places = offsets[:, i * OFFS_COLS : (i + 1) * OFFS_COLS]
-            for kb in range(K_BLOCKS):
-                nc.tensor.matmul(
-                    window[i, a][:].indirect(places),
-                    w_sb[kb][:, a * P : (a + 1) * P],
-                    x_sb[i, kb][:],
-                    start=False, stop=(kb == K_BLOCKS - 1),
-                )
+        def scatter(i, a, kb):
+            nc.tensor.matmul(
+                window[i, a][:].indirect(offsets[:, i * OFFS_COLS : (i + 1) * OFFS_COLS]),
+                w_sb[kb][:, a * P : (a + 1) * P],
+                x_sb[i, kb][:],
+                start=False, stop=(kb == K_BLOCKS - 1),
+            )
+
+        def finish(i, a):
             result = results.tile([P, TOKENS], F32, name="result")
             nc.scalar.activation(result[:], window[i, a][:], GELU, bias=bias[:, a : a + 1])
             nc.sync.dma_start(out[i, a * P : (a + 1) * P, :], result[:])
+
+        for kb in range(K_BLOCKS):
+            for a in range(FEAT_BLOCKS):
+                scatter(0, a, kb)
+        for a in range(FEAT_BLOCKS):
+            finish(0, a)
+        for a in range(FEAT_BLOCKS):
+            for kb in range(K_BLOCKS):
+                scatter(1, a, kb)
+            finish(1, a)

@@ -12,7 +12,7 @@ K_BLOCKS = K // P
 FEAT_BLOCKS = FEATS // P
 OFFS_COLS = PIECE // 16
 
-WARM_UPS = 4
+WARM_UPS = 3
 
 FLOPS = 2 * K * FEATS * N
 

@@ -27,9 +27,6 @@ def tile_scatter_matmul_kernel(tc, base, x, w, b, offs, out):
     ):
         offsets = held.tile([P, N // 16], U16, name="offsets")
 
-        ident = held.tile([P, P], BF16, name="ident")
-        make_identity(nc, ident[:])
-
         base_sb = {(i, a): held.tile([P, TOKENS], BF16, name="base_sb_%d_%d" % (i, a)) for i, a in blocks}
         w_sb = [held.tile([P, FEATS], BF16, name="w_sb_%d" % kb) for kb in range(K_BLOCKS)]
         x_sb = {
@@ -50,6 +47,9 @@ def tile_scatter_matmul_kernel(tc, base, x, w, b, offs, out):
 
         zeros = held.tile([P, TOKENS], BF16, name="zeros")
         nc.vector.memset(zeros[:], 0.0)
+        ident = held.tile([P, P], BF16, name="ident")
+        nc.vector.memset(ident[:], 0.0)
+        make_identity(nc, ident[:], nomemset=True)
         idle_gelu = held.tile([P, 1], F32, name="idle_gelu")
         nc.scalar.activation(idle_gelu[:], zeros[:, 0:1], GELU)
         idle_bank = windows.tile([P, TOKENS], F32, name="idle_bank")

@@ -12,7 +12,7 @@ K_BLOCKS = K // P
 FEAT_BLOCKS = FEATS // P
 OFFS_COLS = PIECE // 16
 
-WARM_UPS = 3
+WARM_UPS = 2
 
 FLOPS = 2 * K * FEATS * N
 

@@ -13,6 +13,7 @@ FEAT_BLOCKS = FEATS // P
 OFFS_COLS = PIECE // 16
 
 WARM_UPS = 2
+DMA_ALIGN = 256
 
 FLOPS = 2 * K * FEATS * N
 
@@ -27,10 +28,15 @@ def tile_scatter_matmul_kernel(tc, base, x, w, b, offs, out):
     ):
         offsets = held.tile([P, N // 16], U16, name="offsets")
 
-        base_sb = {(i, a): held.tile([P, TOKENS], BF16, name="base_sb_%d_%d" % (i, a)) for i, a in blocks}
-        w_sb = [held.tile([P, FEATS], BF16, name="w_sb_%d" % kb) for kb in range(K_BLOCKS)]
+        base_sb = {
+            (i, a): held.tile([P, TOKENS], BF16, name="base_sb_%d_%d" % (i, a), align_bytes=DMA_ALIGN)
+            for i, a in blocks
+        }
+        w_sb = [
+            held.tile([P, FEATS], BF16, name="w_sb_%d" % kb, align_bytes=DMA_ALIGN) for kb in range(K_BLOCKS)
+        ]
         x_sb = {
-            (i, kb): held.tile([P, PIECE], BF16, name="x_sb_%d_%d" % (i, kb))
+            (i, kb): held.tile([P, PIECE], BF16, name="x_sb_%d_%d" % (i, kb), align_bytes=DMA_ALIGN)
             for i in range(SEQS) for kb in range(K_BLOCKS)
         }
         loads = [(base_sb[i, a], base[i, a * P : (a + 1) * P, :]) for i, a in blocks]
@@ -70,7 +76,7 @@ def tile_scatter_matmul_kernel(tc, base, x, w, b, offs, out):
             )
 
         def finish(i, a):
-            result = results.tile([P, TOKENS], F32, name="result")
+            result = results.tile([P, TOKENS], F32, name="result", align_bytes=DMA_ALIGN)
             nc.scalar.activation(result[:], window[i, a][:], GELU, bias=bias[:, a : a + 1])
             nc.sync.dma_start(out[i, a * P : (a + 1) * P, :], result[:])
 

@@ -12,7 +12,7 @@ K_BLOCKS = K // P
 FEAT_BLOCKS = FEATS // P
 OFFS_COLS = PIECE // 16
 
-WARM_UPS = 2
+WARM_UPS = 8
 DMA_ALIGN = 256
 
 FLOPS = 2 * K * FEATS * N
@@ -51,16 +51,16 @@ def tile_scatter_matmul_kernel(tc, base, x, w, b, offs, out):
         for tile, source in loads:
             nc.sync.dma_start(tile[:], source)
 
-        zeros = held.tile([P, TOKENS], BF16, name="zeros")
+        zeros = held.tile([P, P], BF16, name="zeros")
         nc.vector.memset(zeros[:], 0.0)
         ident = held.tile([P, P], BF16, name="ident")
         nc.vector.memset(ident[:], 0.0)
         make_identity(nc, ident[:], nomemset=True)
         idle_gelu = held.tile([P, 1], F32, name="idle_gelu")
         nc.scalar.activation(idle_gelu[:], zeros[:, 0:1], GELU)
-        idle_bank = windows.tile([P, TOKENS], F32, name="idle_bank")
+        idle_bank = windows.tile([P, P], F32, name="idle_bank")
         for repeat in range(WARM_UPS):
-            nc.tensor.matmul(idle_bank[:], zeros[:, 0:P], zeros[:], start=True, stop=True)
+            nc.tensor.matmul(idle_bank[:], zeros[:], zeros[:], start=True, stop=True)
 
         window = {}
         for i, a in blocks:

@@ -76,7 +76,7 @@ def tile_scatter_matmul_kernel(tc, base, x, w, b, offs, out):
             )
 
         def finish(i, a):
-            result = results.tile([P, TOKENS], F32, name="result", align_bytes=DMA_ALIGN)
+            result = results.tile([P, TOKENS], F32, name="result")
             nc.scalar.activation(result[:], window[i, a][:], GELU, bias=bias[:, a : a + 1])
             nc.sync.dma_start(out[i, a * P : (a + 1) * P, :], result[:])
 

@@ -35,19 +35,16 @@ def tile_scatter_matmul_kernel(tc, base, x, w, b, offs, out):
         w_sb = [
             held.tile([P, FEATS], BF16, name="w_sb_%d" % kb, align_bytes=DMA_ALIGN) for kb in range(K_BLOCKS)
         ]
-        x_sb = {
-            (i, kb): held.tile([P, PIECE], BF16, name="x_sb_%d_%d" % (i, kb), align_bytes=DMA_ALIGN)
-            for i in range(SEQS) for kb in range(K_BLOCKS)
-        }
+        x_sb = [
+            held.tile([P, N], BF16, name="x_sb_%d" % kb, align_bytes=DMA_ALIGN) for kb in range(K_BLOCKS)
+        ]
         loads = [(base_sb[i, a], base[i, a * P : (a + 1) * P, :]) for i, a in blocks]
         loads.append((offsets, offs))
         for kb in range(K_BLOCKS):
             loads.append((w_sb[kb], w[kb * P : (kb + 1) * P, :]))
-            loads.append((x_sb[0, kb], x[kb * P : (kb + 1) * P, 0:PIECE]))
+            loads.append((x_sb[kb], x[kb * P : (kb + 1) * P, :]))
         bias = held.tile([P, FEAT_BLOCKS], F32, name="bias")
         loads.append((bias, b.rearrange("(a p) o -> p (a o)", p=P)))
-        for kb in range(K_BLOCKS):
-            loads.append((x_sb[1, kb], x[kb * P : (kb + 1) * P, PIECE : 2 * PIECE]))
         for tile, source in loads:
             nc.sync.dma_start(tile[:], source)
 
@@ -71,7 +68,7 @@ def tile_scatter_matmul_kernel(tc, base, x, w, b, offs, out):
             nc.tensor.matmul(
                 window[i, a][:].indirect(offsets[:, i * OFFS_COLS : (i + 1) * OFFS_COLS]),
                 w_sb[kb][:, a * P : (a + 1) * P],
-                x_sb[i, kb][:],
+                x_sb[kb][:, i * PIECE : (i + 1) * PIECE],
                 start=False, stop=(kb == K_BLOCKS - 1),
             )
 

@@ -38,15 +38,18 @@ def tile_scatter_matmul_kernel(tc, base, x, w, b, offs, out):
         x_sb = [
             held.tile([P, N], BF16, name="x_sb_%d" % kb, align_bytes=DMA_ALIGN) for kb in range(K_BLOCKS)
         ]
-        loads = [(base_sb[i, a], base[i, a * P : (a + 1) * P, :]) for i, a in blocks]
-        loads.append((offsets, offs))
-        for kb in range(K_BLOCKS):
-            loads.append((w_sb[kb], w[kb * P : (kb + 1) * P, :]))
-            loads.append((x_sb[kb], x[kb * P : (kb + 1) * P, :]))
+        loads = [(base_sb[i, a][:], base[i, a * P : (a + 1) * P, :]) for i, a in blocks]
+        loads.append((offsets[:], offs))
+        loads.append((w_sb[0][:], w[0:P, :]))
+        loads.append((x_sb[0][:, 0:PIECE], x[0:P, 0:PIECE]))
+        for kb in range(1, K_BLOCKS):
+            loads.append((w_sb[kb][:], w[kb * P : (kb + 1) * P, :]))
+            loads.append((x_sb[kb][:], x[kb * P : (kb + 1) * P, :]))
+        loads.append((x_sb[0][:, PIECE:N], x[0:P, PIECE:N]))
         bias = held.tile([P, FEAT_BLOCKS], F32, name="bias")
-        loads.append((bias, b.rearrange("(a p) o -> p (a o)", p=P)))
-        for tile, source in loads:
-            nc.sync.dma_start(tile[:], source)
+        loads.append((bias[:], b.rearrange("(a p) o -> p (a o)", p=P)))
+        for target, source in loads:
+            nc.sync.dma_start(target, source)
 
         zeros = held.tile([P, P], BF16, name="zeros")
         nc.vector.memset(zeros[:], 0.0)

import concourse.mybir as mybir
from concourse.masks import make_identity

BF16, F32, U16 = mybir.dt.bfloat16, mybir.dt.float32, mybir.dt.uint16
GELU = mybir.ActivationFunctionType.Gelu_apprx_tanh

P = 128
SEQS, FEATS, TOKENS = 2, 256, 512
K, N = 512, 512
PIECE = N // SEQS
K_BLOCKS = K // P
FEAT_BLOCKS = FEATS // P
OFFS_COLS = PIECE // 16

WARM_UPS = 8
DMA_ALIGN = 256

FLOPS = 2 * K * FEATS * N


def tile_scatter_matmul_kernel(tc, base, x, w, b, offs, out):
    nc = tc.nc
    blocks = [(i, a) for i in range(SEQS) for a in range(FEAT_BLOCKS)]
    with (
        tc.tile_pool(name="held", bufs=1) as held,
        tc.tile_pool(name="results", bufs=SEQS * FEAT_BLOCKS) as results,
        tc.psum_pool(name="windows", bufs=1) as windows,
    ):
        offsets = held.tile([P, N // 16], U16, name="offsets")

        base_sb = {
            (i, a): held.tile([P, TOKENS], BF16, name="base_sb_%d_%d" % (i, a), align_bytes=DMA_ALIGN)
            for i, a in blocks
        }
        w_sb = [
            held.tile([P, FEATS], BF16, name="w_sb_%d" % kb, align_bytes=DMA_ALIGN) for kb in range(K_BLOCKS)
        ]
        x_sb = [
            held.tile([P, N], BF16, name="x_sb_%d" % kb, align_bytes=DMA_ALIGN) for kb in range(K_BLOCKS)
        ]
        loads = [(base_sb[i, a][:], base[i, a * P : (a + 1) * P, :]) for i, a in blocks]
        loads.append((offsets[:], offs))
        loads.append((w_sb[0][:], w[0:P, :]))
        loads.append((x_sb[0][:, 0:PIECE], x[0:P, 0:PIECE]))
        for kb in range(1, K_BLOCKS):
            loads.append((w_sb[kb][:], w[kb * P : (kb + 1) * P, :]))
            loads.append((x_sb[kb][:], x[kb * P : (kb + 1) * P, :]))
        loads.append((x_sb[0][:, PIECE:N], x[0:P, PIECE:N]))
        bias = held.tile([P, FEAT_BLOCKS], F32, name="bias")
        loads.append((bias[:], b.rearrange("(a p) o -> p (a o)", p=P)))
        for target, source in loads:
            nc.sync.dma_start(target, source)

        zeros = held.tile([P, P], BF16, name="zeros")
        nc.vector.memset(zeros[:], 0.0)
        ident = held.tile([P, P], BF16, name="ident")
        nc.vector.memset(ident[:], 0.0)
        make_identity(nc, ident[:], nomemset=True)
        idle_gelu = held.tile([P, 1], F32, name="idle_gelu")
        nc.scalar.activation(idle_gelu[:], zeros[:, 0:1], GELU)
        idle_bank = windows.tile([P, P], F32, name="idle_bank")
        for repeat in range(WARM_UPS):
            nc.tensor.matmul(idle_bank[:], zeros[:], zeros[:], start=True, stop=True)

        window = {}
        for i, a in blocks:
            window[i, a] = windows.tile([P, TOKENS], F32, name="window_%d_%d" % (i, a))
            nc.tensor.matmul(window[i, a][:], ident[:], base_sb[i, a][:], start=True, stop=False)

        def scatter(i, a, kb):
            nc.tensor.matmul(
                window[i, a][:].indirect(offsets[:, i * OFFS_COLS : (i + 1) * OFFS_COLS]),
                w_sb[kb][:, a * P : (a + 1) * P],
                x_sb[kb][:, i * PIECE : (i + 1) * PIECE],
                start=False, stop=(kb == K_BLOCKS - 1),
            )

        def finish(i, a):
            result = results.tile([P, TOKENS], F32, name="result")
            nc.scalar.activation(result[:], window[i, a][:], GELU, bias=bias[:, a : a + 1])
            nc.sync.dma_start(out[i, a * P : (a + 1) * P, :], result[:])

        for kb in range(K_BLOCKS):
            for a in range(FEAT_BLOCKS):
                scatter(0, a, kb)
        for a in range(FEAT_BLOCKS):
            finish(0, a)
        for a in range(FEAT_BLOCKS):
            for kb in range(K_BLOCKS):
                scatter(1, a, kb)
            finish(1, a)
